import numpy as np
import ml_dtypes


def mxq(x, axis, fmt="e4m3"):
    dtype, down = {"e4m3": (ml_dtypes.float8_e4m3fn, 7), "e5m2": (ml_dtypes.float8_e5m2, 14)}[fmt]
    v = np.moveaxis(np.asarray(x, np.float32).astype(ml_dtypes.bfloat16).astype(np.float64), axis, -1)
    blocks = v.reshape(v.shape[:-1] + (-1, 32))
    amax = np.abs(blocks).max(-1, keepdims=True)
    byte = np.maximum(np.where(amax > 0, np.frexp(amax)[1] - 1 + 127, 0) - down, 1)
    scale = np.exp2(byte - 127.0)
    codes = (blocks / scale).astype(np.float32).astype(dtype).astype(np.float64)
    return np.moveaxis((codes * scale).reshape(v.shape), -1, axis)


WIDE = False


def mx_kscale(k):
    if not WIDE:
        return np.ones(k)
    levels = np.array([30, -30])
    if k % 512:
        return np.exp2(np.random.permutation(np.resize(levels, k // 32))).repeat(32)
    a = np.empty((k // 512, 16))
    for p in range(k // 512):
        a[p, :8] = np.random.permutation(np.resize(levels, 8))
        for g in range(8):
            far = levels[np.abs(levels - a[p, g]) >= 10]
            a[p, g + 8] = far[np.random.randint(len(far))]
    return np.exp2(a.ravel()).repeat(32)


def f64(x):
    return np.asarray(x).astype(np.float64)


def striped(idx):
    return np.tile(np.asarray(idx).reshape(-1, 16).T, (8, 1)).astype(np.uint16)


def unstriped(offs):
    return offs[:16].T.reshape(-1).astype(np.int64)


def striped8(idx):
    return np.asarray(idx).reshape(8, -1, 16).transpose(0, 2, 1).reshape(128, -1).astype(np.uint16)


def unstriped8(offs):
    return offs.reshape(8, 16, -1).transpose(0, 2, 1).reshape(8, -1).astype(np.int64)


def pick8(x, idx, run):
    r = np.arange(len(x))
    return x[r[:, None], idx[r % (8 * run) // run]]


E2M1 = np.array([0.0, 0.5, 1.0, 1.5, 2.0, 3.0, 4.0, 6.0, -0.0, -0.5, -1.0, -1.5, -2.0, -3.0, -4.0, -6.0])


def pack_weight(w, fmt):
    k, n = w.shape
    w = f64(np.asarray(w, np.float32).astype(ml_dtypes.bfloat16)).reshape(k // 32, 32, n)
    amax = np.abs(w).max(1)
    if fmt in ("e4m3", "e5m2"):
        byte = np.frexp(amax)[1] - 1 + 127 - (7 if fmt == "e4m3" else 14)
    else:
        mant, ex = np.frexp(amax / 6.0)
        byte = np.where(mant > 0.5, ex, ex - 1) + 127
    byte = np.clip(np.where(amax > 0, byte, 1), 1, 254)
    scaled = (w * np.exp2(127.0 - byte)[:, None, :]).reshape(k, n).astype(np.float32)
    by_word = np.ascontiguousarray(scaled.reshape(k // 512, 128, 4, n).transpose(0, 1, 3, 2))
    if fmt in ("e4m3", "e5m2"):
        words = by_word.astype(ml_dtypes.float8_e4m3fn if fmt == "e4m3" else ml_dtypes.float8_e5m2).view(np.uint8)
    else:
        c = by_word.astype(ml_dtypes.float4_e2m1fn).view(np.uint8) & 0xF
        words = (c[..., 0::2] | (c[..., 1::2] << 4)).reshape(k // 512, 128, 2 * n)
    return np.ascontiguousarray(words), np.ascontiguousarray(byte.astype(np.uint8).reshape(k // 512, 16, n))


def unpack_weight(words, scales, fmt):
    g, _, n = scales.shape
    words = np.ascontiguousarray(words).reshape(g, 128, n, -1)
    if fmt in ("e4m3", "e5m2"):
        vals = words.view(ml_dtypes.float8_e4m3fn if fmt == "e4m3" else ml_dtypes.float8_e5m2).astype(np.float64)
    else:
        nib = np.empty((g, 128, n, 4), np.uint8)
        nib[..., 0::2] = words & 0xF
        nib[..., 1::2] = words >> 4
        vals = E2M1[nib]
    vals = vals * np.repeat(np.exp2(scales.astype(np.float64) - 127.0), 8, axis=1)[..., None]
    return vals.transpose(0, 1, 3, 2).reshape(g * 512, n)


K, T, J, R, C, O, N, S, E = 512, 1024, 256, 512, 512, 128, 256, 1024, 512


def setup_inputs():
    n = np.random.standard_normal
    idx = np.random.permutation(T)[:J]
    idx2 = np.stack([np.random.permutation(C)[:J] for _ in range(8)])
    idx3 = np.stack([np.random.permutation(C)[:O] for _ in range(8)])
    idx4 = np.stack([np.random.permutation(C)[:O] for _ in range(8)])
    idx5 = np.random.permutation(S)[:N]
    idx6 = np.stack([np.random.permutation(E)[:O] for _ in range(8)])
    idx7 = np.random.permutation(E)[:O]
    fk = mx_kscale(K)
    fr = mx_kscale(R)
    xtp = pack_weight(n((K, T)) / fk[:, None], "e4m3")
    wp = pack_weight(n((K, R)) * 1 / np.sqrt(K) * fk[:, None] * fr, "e2m1")
    vsp = pack_weight(n((R, S)) * 1 / np.sqrt(R) / fr[:, None], "e5m2")
    return {
        "xt_words": xtp[0],
        "xt_scales": xtp[1],
        "w_words": wp[0],
        "w_scales": wp[1],
        "sa": (np.random.uniform(0.5, 1.6, (R, 1))).astype(np.float32),
        "sb": (np.random.uniform(0.5, 1.6, (R, 1))).astype(np.float32),
        "vs_words": vsp[0],
        "vs_scales": vsp[1],
        "offs": striped(idx),
        "offs2": striped8(idx2),
        "offs3": striped8(idx3),
        "offs4": striped8(idx4),
        "offs5": striped(idx5),
        "offs6": striped8(idx6),
        "offs7": striped(idx7),
    }


def reference(xt_words, xt_scales, w_words, w_scales, sa, sb, vs_words, vs_scales, offs, offs2, offs3, offs4, offs5, offs6, offs7):
    idx = unstriped(offs)
    idx2 = unstriped8(offs2)
    idx3 = unstriped8(offs3)
    idx4 = unstriped8(offs4)
    idx5 = unstriped(offs5)
    idx6 = unstriped8(offs6)
    idx7 = unstriped(offs7)
    xtu = unpack_weight(xt_words, xt_scales, "e4m3")
    wu = unpack_weight(w_words, w_scales, "e2m1")
    vsu = unpack_weight(vs_words, vs_scales, "e5m2")
    xtidxg = xtu[:, idx]
    a = wu.T @ xtidxg
    pw = np.zeros((R, C))
    pw[np.arange(R)[:, None], idx2[np.arange(R) % 512 // 64]] = a
    hid = np.abs(pick8(pw, idx3, 64) * f64(sa) - pick8(pw, idx4, 64) * f64(sb))
    vsidx5g = vsu[:, idx5]
    hidq = mxq(hid, 0, "e4m3")
    p = vsidx5g.T @ hidq
    pa = np.zeros((N, E))
    pa[np.arange(N)[:, None], idx6[np.arange(N) % 128 // 16]] = p
    pb = np.zeros((N, E))
    pb[:, idx7] = p
    y = pa + pb
    return y

@@ -1,0 +1,227 @@
+from contextlib import ExitStack
+
+import concourse.mybir as mybir
+
+K, T, J, R, C, O, N, S, E = 512, 1024, 256, 512, 512, 128, 256, 1024, 512
+FLOPS = 2 * K * R * J + 2 * R * N * O
+
+F32 = mybir.dt.float32
+BF16 = mybir.dt.bfloat16
+I32 = mybir.dt.int32
+U32 = mybir.dt.uint32
+U16 = mybir.dt.uint16
+U8 = mybir.dt.uint8
+E4M3X4 = mybir.dt.float8_e4m3fn_x4
+E5M2X4 = mybir.dt.float8_e5m2_x4
+E2M1X4 = mybir.dt.float4_e2m1fn_x4
+ALU = mybir.AluOpType
+COPY = mybir.ActivationFunctionType.Copy
+
+P = 128
+PACK = 4
+HALF = J // 2
+
+
+def tile_list_ownreads_solo_store_owntwopages_kernel(
+    tc, xt_words, xt_scales, w_words, w_scales, sa, sb, vs_words, vs_scales,
+    offs, offs2, offs3, offs4, offs5, offs6, offs7, out,
+):
+    nc = tc.nc
+    with ExitStack() as ctx:
+        lists = ctx.enter_context(tc.tile_pool(name="lists", bufs=1))
+        sbuf = ctx.enter_context(tc.tile_pool(name="sbuf", bufs=1))
+        x_room = ctx.enter_context(tc.tile_pool(name="x_room", bufs=1))
+        v_room = ctx.enter_context(tc.tile_pool(name="v_room", bufs=1))
+        psum = ctx.enter_context(tc.psum_pool(name="psum", bufs=1))
+
+        def load_list(name, source):
+            tile = lists.tile([P, source.shape[1]], U16, name=name)
+            nc.sync.dma_start(tile[:], source)
+            return tile
+
+        def load_scale_rows(name, source, queues):
+            width = source.shape[2] // 4
+            staged = sbuf.tile([P, 2, width], I32, name=name)
+            rows = source[0].bitcast(I32)
+            for h in range(2):
+                queues[h].dma_start(
+                    staged[64 * h : 64 * h + 4, :, :],
+                    rows[8 * h : 8 * h + 8, :].rearrange("(q r) n -> r q n", q=2),
+                )
+            return staged
+
+        def spread_scale_rows(name, staged, in_place_copy):
+            width = staged.shape[2]
+            plane = sbuf.tile([P, 4 * width], U8, name=name, tag=name, align_bytes=64)
+            nc.vector.memset(plane[:].bitcast(I32), 0)
+            for h in range(2):
+                rows = slice(64 * h, 64 * h + 4)
+                in_place_copy(plane[:].bitcast(U32)[rows, :], staged[rows, 0, :].bitcast(U32))
+                nc.vector.tensor_copy(plane[:].bitcast(I32)[64 * h + 32 : 64 * h + 36, :], staged[rows, 1, :])
+            return plane
+
+        def load_words(name, source, room):
+            tile = room.tile([P, source.shape[2]], I32, name=name, offset=0)
+            nc.sync.dma_start(tile[:], source[0].rearrange("p n t -> p (n t)").bitcast(I32))
+            return tile
+
+        ws_staged = load_scale_rows("ws_staged", w_scales, (nc.scalar, nc.sync))
+        xs_staged = load_scale_rows("xs_staged", xt_scales, (nc.scalar, nc.sync))
+        tokens = load_list("tokens", offs)
+        w_raw = sbuf.tile([P, 2 * R], U8, name="w_raw", tag="w_raw")
+        nc.sync.dma_start(w_raw[:].bitcast(I32), w_words[0].bitcast(I32))
+        x_raw = load_words("x_raw", xt_words, x_room)
+        put = load_list("put", offs2)
+        pick_a = load_list("pick_a", offs3)
+        sa_sb = sbuf.tile([P, PACK], F32, name="sa_sb")
+        sb_sb = sbuf.tile([P, PACK], F32, name="sb_sb")
+        nc.sync.dma_start(sa_sb[:], sa.rearrange("(p t) o -> p (t o)", t=PACK))
+        pick_b = load_list("pick_b", offs4)
+        nc.sync.dma_start(sb_sb[:], sb.rearrange("(p t) o -> p (t o)", t=PACK))
+        entries = load_list("entries", offs5)
+        v_raw = load_words("v_raw", vs_words, v_room)
+        vs_plane = sbuf.tile([P, S], U8, name="vs_plane", align_bytes=64)
+        nc.vector.memset(vs_plane[:].bitcast(I32), 0)
+        for q in range(4):
+            nc.sync.dma_start(
+                vs_plane[:].bitcast(I32)[32 * q : 32 * q + 4, :], vs_scales[0].bitcast(I32)[4 * q : 4 * q + 4, :]
+            )
+        own = load_list("own", offs6)
+        common = load_list("common", offs7)
+
+        ws_plane = spread_scale_rows("ws_plane", ws_staged, nc.vector.tensor_copy)
+        xs_plane = spread_scale_rows("xs_plane", xs_staged, nc.vector.tensor_copy)
+        boards = []
+
+        def clear_board(board):
+            nc.vector.memset(board[:], 0.0)
+            boards.append(board)
+
+        for t in range(2):
+            clear_board(sbuf.tile([P, C], F32, name="board%d" % t, tag="board%d" % t))
+
+        w_dealt = sbuf.tile([P, 2 * R], U8, name="w_dealt", align_bytes=64)
+        ws_dealt = sbuf.tile([P, R], U8, name="ws_dealt", align_bytes=64)
+        x_got = sbuf.tile([P, J], U32, name="x_got", tag="got_words", align_bytes=64)
+        xs_got = sbuf.tile([P, J], U8, name="xs_got", tag="got_scales", align_bytes=64)
+        a_sb = [sbuf.tile([P, J], F32, name="a_sb%d" % t, tag="rows%d" % t, align_bytes=64) for t in range(PACK - 1)]
+
+        def deal(t0):
+            nc.scalar.copy(
+                w_dealt[:].bitcast(U16).rearrange("p (t m) -> p t m", t=PACK)[:, t0 : t0 + 2, :],
+                w_raw[:].bitcast(U16).rearrange("p (m t) -> p t m", t=PACK)[:, t0 : t0 + 2, :],
+            )
+            nc.vector.tensor_copy(
+                ws_dealt[:].rearrange("p (t m) -> p t m", t=PACK)[:, t0 : t0 + 2, :],
+                ws_plane[:].rearrange("p (m t) -> p t m", t=PACK)[:, t0 : t0 + 2, :],
+            )
+
+        def gather_tokens(lo, hi):
+            at = tokens[:, lo // 16 : hi // 16]
+            nc.vector.tensor_copy(xs_got[:, lo:hi], xs_plane[:].indirect(at))
+            nc.vector.tensor_copy(x_got[:, lo:hi], x_raw[:].bitcast(U32).indirect(at))
+
+        def first_product(t, lo, hi, emptier):
+            acc = psum.tile([P, hi - lo], F32, name="acc%d_%d" % (t, lo))
+            nc.tensor.matmul_mx(
+                out=acc[:],
+                lhsT=w_dealt[:, 2 * P * t : 2 * P * (t + 1)].bitcast(E2M1X4),
+                lhsT_scale=ws_dealt[:, P * t : P * (t + 1)],
+                rhs=x_got[:, lo:hi].bitcast(E4M3X4),
+                rhs_scale=xs_got[:, lo:hi],
+                start=True,
+                stop=True,
+            )
+            if emptier is not None:
+                emptier(a_sb[t][:, lo:hi], acc[:])
+            return acc
+
+        def put_on_board(t, lo, hi):
+            nc.scalar.activation(boards[t][:].indirect(put[:, lo // 16 : hi // 16]), a_sb[t][:, lo:hi], COPY)
+
+        deal(0)
+        gather_tokens(0, HALF)
+        for t in range(2):
+            first_product(t, 0, HALF, nc.scalar.copy)
+        gather_tokens(HALF, J)
+        deal(2)
+        for t in range(2):
+            put_on_board(t, 0, HALF)
+        for t in range(2):
+            first_product(t, HALF, J, nc.vector.tensor_copy)
+            put_on_board(t, HALF, J)
+        for t in range(2, PACK):
+            last_acc = first_product(t, 0, J, nc.vector.tensor_copy if t == 2 else None)
+            clear_board(x_room.tile([P, C], F32, name="board%d" % t, offset=4 * C * (t - 2)))
+
+        v_got = sbuf.tile([P, N], U32, name="v_got", tag="got_words", align_bytes=64)
+        vs_got = sbuf.tile([P, N], U8, name="vs_got", tag="got_scales", align_bytes=64)
+        nc.vector.tensor_copy(vs_got[:], vs_plane[:].indirect(entries[:]))
+        nc.vector.tensor_copy(v_got[:], v_raw[:].bitcast(U32).indirect(entries[:]))
+
+        hid = sbuf.tile([P, O, PACK], BF16, name="hid", align_bytes=64)
+        pages = []
+
+        def clear_page(page):
+            nc.vector.memset(page[:], 0.0)
+            pages.append(page)
+
+        def read_board(t):
+            left = sbuf.tile([P, O], F32, name="left%d" % t)
+            right = sbuf.tile([P, O], F32, name="right%d" % t)
+            gap = v_room.tile([P, O], F32, name="gap%d" % t, offset=0)
+            nc.scalar.activation(left[:], boards[t][:].indirect(pick_a[:]), COPY, scale=sa_sb[:, t : t + 1])
+            nc.scalar.activation(right[:], boards[t][:].indirect(pick_b[:]), COPY, scale=sb_sb[:, t : t + 1])
+            nc.vector.tensor_tensor(gap[:], left[:], right[:], ALU.subtract)
+            nc.vector.scalar_tensor_tensor(hid[:, :, t], gap[:], -1.0, gap[:], ALU.mult, ALU.max)
+            return right
+
+        for t in range(2):
+            clear_page(v_room.tile([P, E], F32, name="page%d" % t, offset=4 * O + 4 * E * t))
+        for t in range(2):
+            clear_page(sbuf.tile([P, E], F32, name="page%d" % (t + 2), tag="rows%d" % t, align_bytes=64))
+        put_on_board(2, 0, J)
+        read_board(0)
+        a_sb.append(sbuf.tile([P, J], F32, name="a_sb3", tag="board0"))
+        nc.vector.tensor_copy(a_sb[3][:], last_acc[:])
+        read_board(1)
+        put_on_board(3, 0, J)
+        read_board(2)
+        right = read_board(3)
+
+        hid_codes = sbuf.tile([P, O], U32, name="hid_codes", align_bytes=64)
+        hid_scales = sbuf.tile([P, O], U8, name="hid_scales", align_bytes=64)
+        nc.vector.quantize_mx(
+            out=hid_codes[:].bitcast(E4M3X4), scales=hid_scales[:], in_=hid[:].rearrange("p o t -> p (o t)")
+        )
+
+        results = []
+        for c, emptier in enumerate((nc.scalar.copy, nc.vector.tensor_copy)):
+            acc = psum.tile([P, O], F32, name="res%d" % c)
+            nc.tensor.matmul_mx(
+                out=acc[:],
+                lhsT=v_got[:, P * c : P * (c + 1)].bitcast(E5M2X4),
+                lhsT_scale=vs_got[:, P * c : P * (c + 1)],
+                rhs=hid_codes[:].bitcast(E4M3X4),
+                rhs_scale=hid_scales[:],
+                start=True,
+                stop=True,
+            )
+            result = sbuf.tile([P, O], F32, name="result%d" % c)
+            emptier(result[:], acc[:])
+            results.append(result)
+        totals = [sbuf.tile([P, E], F32, name="total%d" % c) for c in range(2)]
+
+        def add_and_store(c, pieces):
+            for lo in range(0, E, E // pieces):
+                cols = slice(lo, lo + E // pieces)
+                nc.vector.tensor_tensor(totals[c][:, cols], pages[2 * c][:, cols], pages[2 * c + 1][:, cols], ALU.add)
+                nc.sync.dma_start(out[P * c : P * (c + 1), cols], totals[c][:, cols])
+
+        nc.scalar.activation(pages[0][:].indirect(own[:]), results[0][:], COPY)
+        nc.vector.tensor_copy(pages[1][:].indirect(common[:]), results[0][:])
+        nc.vector.tensor_copy(pages[3][:].indirect(common[:, 0:4]), results[1][:, 0:64])
+        nc.scalar.activation(pages[2][:].indirect(own[:]), results[1][:], COPY)
+        nc.scalar.activation(pages[3][:].indirect(common[:, 4:8]), results[1][:, 64:128], COPY)
+        add_and_store(0, 1)
+        add_and_store(1, 2)

@@ -60,8 +60,8 @@ def tile_list_ownreads_solo_store_owntwopages_kernel(
                 nc.vector.tensor_copy(plane[:].bitcast(I32)[64 * h + 32 : 64 * h + 36, :], staged[rows, 1, :])
             return plane
 
-        def load_words(name, source, room):
-            tile = room.tile([P, source.shape[2]], I32, name=name, offset=0)
+        def load_words(name, source, room, offset):
+            tile = room.tile([P, source.shape[2]], I32, name=name, offset=offset)
             nc.sync.dma_start(tile[:], source[0].rearrange("p n t -> p (n t)").bitcast(I32))
             return tile
 
@@ -70,22 +70,22 @@ def tile_list_ownreads_solo_store_owntwopages_kernel(
         tokens = load_list("tokens", offs)
         w_raw = sbuf.tile([P, 2 * R], U8, name="w_raw", tag="w_raw")
         nc.sync.dma_start(w_raw[:].bitcast(I32), w_words[0].bitcast(I32))
-        x_raw = load_words("x_raw", xt_words, x_room)
+        x_raw = load_words("x_raw", xt_words, x_room, 1024)
         put = load_list("put", offs2)
         pick_a = load_list("pick_a", offs3)
+        pick_b = load_list("pick_b", offs4)
         sa_sb = sbuf.tile([P, PACK], F32, name="sa_sb")
         sb_sb = sbuf.tile([P, PACK], F32, name="sb_sb")
         nc.sync.dma_start(sa_sb[:], sa.rearrange("(p t) o -> p (t o)", t=PACK))
-        pick_b = load_list("pick_b", offs4)
         nc.sync.dma_start(sb_sb[:], sb.rearrange("(p t) o -> p (t o)", t=PACK))
         entries = load_list("entries", offs5)
-        v_raw = load_words("v_raw", vs_words, v_room)
-        vs_plane = sbuf.tile([P, S], U8, name="vs_plane", align_bytes=64)
+        vs_plane = sbuf.tile([P, S], U8, name="vs_plane", tag="vs_plane", align_bytes=64)
         nc.vector.memset(vs_plane[:].bitcast(I32), 0)
         for q in range(4):
             nc.sync.dma_start(
                 vs_plane[:].bitcast(I32)[32 * q : 32 * q + 4, :], vs_scales[0].bitcast(I32)[4 * q : 4 * q + 4, :]
             )
+        v_raw = load_words("v_raw", vs_words, v_room, 0)
         own = load_list("own", offs6)
         common = load_list("common", offs7)
 
@@ -93,27 +93,27 @@ def tile_list_ownreads_solo_store_owntwopages_kernel(
         xs_plane = spread_scale_rows("xs_plane", xs_staged, nc.vector.tensor_copy)
         boards = []
 
-        def clear_board(board):
-            nc.vector.memset(board[:], 0.0)
+        def clear_board(board, engine):
+            engine.memset(board[:], 0.0)
             boards.append(board)
 
         for t in range(2):
-            clear_board(sbuf.tile([P, C], F32, name="board%d" % t, tag="board%d" % t))
+            clear_board(sbuf.tile([P, C], F32, name="board%d" % t), nc.vector)
 
         w_dealt = sbuf.tile([P, 2 * R], U8, name="w_dealt", align_bytes=64)
         ws_dealt = sbuf.tile([P, R], U8, name="ws_dealt", align_bytes=64)
-        x_got = sbuf.tile([P, J], U32, name="x_got", tag="got_words", align_bytes=64)
+        x_got = sbuf.tile([P, J], U32, name="x_got", align_bytes=64)
         xs_got = sbuf.tile([P, J], U8, name="xs_got", tag="got_scales", align_bytes=64)
-        a_sb = [sbuf.tile([P, J], F32, name="a_sb%d" % t, tag="rows%d" % t, align_bytes=64) for t in range(PACK - 1)]
+        a_sb = [sbuf.tile([P, J], F32, name="a_sb%d" % t, tag="rows%d" % t, align_bytes=64) for t in range(PACK)]
 
-        def deal(t0):
+        def deal(t0, t1):
             nc.scalar.copy(
-                w_dealt[:].bitcast(U16).rearrange("p (t m) -> p t m", t=PACK)[:, t0 : t0 + 2, :],
-                w_raw[:].bitcast(U16).rearrange("p (m t) -> p t m", t=PACK)[:, t0 : t0 + 2, :],
+                w_dealt[:].bitcast(U16).rearrange("p (t m) -> p t m", t=PACK)[:, t0:t1, :],
+                w_raw[:].bitcast(U16).rearrange("p (m t) -> p t m", t=PACK)[:, t0:t1, :],
             )
             nc.vector.tensor_copy(
-                ws_dealt[:].rearrange("p (t m) -> p t m", t=PACK)[:, t0 : t0 + 2, :],
-                ws_plane[:].rearrange("p (m t) -> p t m", t=PACK)[:, t0 : t0 + 2, :],
+                ws_dealt[:].rearrange("p (t m) -> p t m", t=PACK)[:, t0:t1, :],
+                ws_plane[:].rearrange("p (m t) -> p t m", t=PACK)[:, t0:t1, :],
             )
 
         def gather_tokens(lo, hi):
@@ -132,29 +132,27 @@ def tile_list_ownreads_solo_store_owntwopages_kernel(
                 start=True,
                 stop=True,
             )
-            if emptier is not None:
-                emptier(a_sb[t][:, lo:hi], acc[:])
-            return acc
+            emptier(a_sb[t][:, lo:hi], acc[:])
 
         def put_on_board(t, lo, hi):
             nc.scalar.activation(boards[t][:].indirect(put[:, lo // 16 : hi // 16]), a_sb[t][:, lo:hi], COPY)
 
-        deal(0)
+        deal(0, 2)
         gather_tokens(0, HALF)
         for t in range(2):
             first_product(t, 0, HALF, nc.scalar.copy)
         gather_tokens(HALF, J)
-        deal(2)
+        deal(2, PACK)
         for t in range(2):
             put_on_board(t, 0, HALF)
         for t in range(2):
             first_product(t, HALF, J, nc.vector.tensor_copy)
             put_on_board(t, HALF, J)
         for t in range(2, PACK):
-            last_acc = first_product(t, 0, J, nc.vector.tensor_copy if t == 2 else None)
-            clear_board(x_room.tile([P, C], F32, name="board%d" % t, offset=4 * C * (t - 2)))
+            first_product(t, 0, J, nc.vector.tensor_copy)
+            clear_board(x_room.tile([P, C], F32, name="board%d" % t, offset=4 * C * (t - 2)), nc.gpsimd)
 
-        v_got = sbuf.tile([P, N], U32, name="v_got", tag="got_words", align_bytes=64)
+        v_got = sbuf.tile([P, N], U32, name="v_got", tag="vs_plane", align_bytes=64)
         vs_got = sbuf.tile([P, N], U8, name="vs_got", tag="got_scales", align_bytes=64)
         nc.vector.tensor_copy(vs_got[:], vs_plane[:].indirect(entries[:]))
         nc.vector.tensor_copy(v_got[:], v_raw[:].bitcast(U32).indirect(entries[:]))
@@ -163,37 +161,50 @@ def tile_list_ownreads_solo_store_owntwopages_kernel(
         pages = []
 
         def clear_page(page):
-            nc.vector.memset(page[:], 0.0)
+            nc.gpsimd.memset(page[:], 0.0)
             pages.append(page)
 
         def read_board(t):
-            left = sbuf.tile([P, O], F32, name="left%d" % t)
-            right = sbuf.tile([P, O], F32, name="right%d" % t)
-            gap = v_room.tile([P, O], F32, name="gap%d" % t, offset=0)
+            left = v_room.tile([P, O], F32, name="left%d" % t, offset=4 * O * 2 * t)
+            right = v_room.tile([P, O], F32, name="right%d" % t, offset=4 * O * (2 * t + 1))
             nc.scalar.activation(left[:], boards[t][:].indirect(pick_a[:]), COPY, scale=sa_sb[:, t : t + 1])
             nc.scalar.activation(right[:], boards[t][:].indirect(pick_b[:]), COPY, scale=sb_sb[:, t : t + 1])
-            nc.vector.tensor_tensor(gap[:], left[:], right[:], ALU.subtract)
-            nc.vector.scalar_tensor_tensor(hid[:, :, t], gap[:], -1.0, gap[:], ALU.mult, ALU.max)
-            return right
+            return left, right
 
+        def difference(t, gaps, picked, cols):
+            nc.vector.tensor_tensor(gaps[:, t % 2, cols], picked[0][:, cols], picked[1][:, cols], ALU.subtract)
+
+        def magnitudes(t0, gaps, cols):
+            pairs = gaps[:].rearrange("p t o -> p o t")[:, cols, :]
+            nc.vector.scalar_tensor_tensor(hid[:, cols, t0 : t0 + 2], pairs, -1.0, pairs, ALU.mult, ALU.max)
+
+        clear_page(x_room.tile([P, E], F32, name="page0", offset=2 * 4 * C))
         for t in range(2):
-            clear_page(v_room.tile([P, E], F32, name="page%d" % t, offset=4 * O + 4 * E * t))
-        for t in range(2):
-            clear_page(sbuf.tile([P, E], F32, name="page%d" % (t + 2), tag="rows%d" % t, align_bytes=64))
+            clear_page(sbuf.tile([P, E], F32, name="page%d" % (t + 1), tag="rows%d" % t, align_bytes=64))
         put_on_board(2, 0, J)
-        read_board(0)
-        a_sb.append(sbuf.tile([P, J], F32, name="a_sb3", tag="board0"))
-        nc.vector.tensor_copy(a_sb[3][:], last_acc[:])
-        read_board(1)
+        clear_page(sbuf.tile([P, E], F32, name="page3", tag="rows2", align_bytes=64))
         put_on_board(3, 0, J)
-        read_board(2)
-        right = read_board(3)
-
+        whole = slice(0, O)
+        halves = (slice(0, O // 2), slice(O // 2, O))
+        gaps = sbuf.tile([P, 2, O], F32, name="gaps01", tag="gaps")
+        for t in range(2):
+            difference(t, gaps, read_board(t), whole)
+        magnitudes(0, gaps, whole)
+        gaps = sbuf.tile([P, 2, O], F32, name="gaps23", tag="gaps")
+        difference(2, gaps, read_board(2), whole)
+        picked = read_board(3)
         hid_codes = sbuf.tile([P, O], U32, name="hid_codes", align_bytes=64)
         hid_scales = sbuf.tile([P, O], U8, name="hid_scales", align_bytes=64)
-        nc.vector.quantize_mx(
-            out=hid_codes[:].bitcast(E4M3X4), scales=hid_scales[:], in_=hid[:].rearrange("p o t -> p (o t)")
-        )
+        for cols in halves:
+            difference(3, gaps, picked, cols)
+        for cols in halves:
+            magnitudes(2, gaps, cols)
+        for cols in halves:
+            nc.vector.quantize_mx(
+                out=hid_codes[:, cols].bitcast(E4M3X4),
+                scales=hid_scales[:, cols],
+                in_=hid[:, cols, :].rearrange("p o t -> p (o t)"),
+            )
 
         results = []
         for c, emptier in enumerate((nc.scalar.copy, nc.vector.tensor_copy)):

@@ -30,7 +30,9 @@ def tile_list_ownreads_solo_store_owntwopages_kernel(
     with ExitStack() as ctx:
         lists = ctx.enter_context(tc.tile_pool(name="lists", bufs=1))
         sbuf = ctx.enter_context(tc.tile_pool(name="sbuf", bufs=1))
-        x_room = ctx.enter_context(tc.tile_pool(name="x_room", bufs=1))
+        w_room = ctx.enter_context(tc.tile_pool(name="w_room", bufs=1))
+        d_room = ctx.enter_context(tc.tile_pool(name="d_room", bufs=1))
+        s_room = ctx.enter_context(tc.tile_pool(name="s_room", bufs=1))
         v_room = ctx.enter_context(tc.tile_pool(name="v_room", bufs=1))
         psum = ctx.enter_context(tc.psum_pool(name="psum", bufs=1))
 
@@ -65,12 +67,12 @@ def tile_list_ownreads_solo_store_owntwopages_kernel(
             nc.sync.dma_start(tile[:], source[0].rearrange("p n t -> p (n t)").bitcast(I32))
             return tile
 
+        tokens = load_list("tokens", offs)
         ws_staged = load_scale_rows("ws_staged", w_scales, (nc.scalar, nc.sync))
         xs_staged = load_scale_rows("xs_staged", xt_scales, (nc.scalar, nc.sync))
-        tokens = load_list("tokens", offs)
-        w_raw = sbuf.tile([P, 2 * R], U8, name="w_raw", tag="w_raw")
+        x_raw = load_words("x_raw", xt_words, sbuf, None)
+        w_raw = w_room.tile([P, 2 * R], U8, name="w_raw", offset=0)
         nc.sync.dma_start(w_raw[:].bitcast(I32), w_words[0].bitcast(I32))
-        x_raw = load_words("x_raw", xt_words, x_room, 1024)
         put = load_list("put", offs2)
         pick_a = load_list("pick_a", offs3)
         pick_b = load_list("pick_b", offs4)
@@ -79,7 +81,7 @@ def tile_list_ownreads_solo_store_owntwopages_kernel(
         nc.sync.dma_start(sa_sb[:], sa.rearrange("(p t) o -> p (t o)", t=PACK))
         nc.sync.dma_start(sb_sb[:], sb.rearrange("(p t) o -> p (t o)", t=PACK))
         entries = load_list("entries", offs5)
-        vs_plane = sbuf.tile([P, S], U8, name="vs_plane", tag="vs_plane", align_bytes=64)
+        vs_plane = s_room.tile([P, S], U8, name="vs_plane", offset=512, align_bytes=64)
         nc.vector.memset(vs_plane[:].bitcast(I32), 0)
         for q in range(4):
             nc.sync.dma_start(
@@ -93,76 +95,90 @@ def tile_list_ownreads_solo_store_owntwopages_kernel(
         xs_plane = spread_scale_rows("xs_plane", xs_staged, nc.vector.tensor_copy)
         boards = []
 
-        def clear_board(board, engine):
-            engine.memset(board[:], 0.0)
+        def clear_board(board):
+            nc.vector.memset(board[:], 0.0)
             boards.append(board)
 
         for t in range(2):
-            clear_board(sbuf.tile([P, C], F32, name="board%d" % t), nc.vector)
+            clear_board(sbuf.tile([P, C], F32, name="board%d" % t))
 
-        w_dealt = sbuf.tile([P, 2 * R], U8, name="w_dealt", align_bytes=64)
-        ws_dealt = sbuf.tile([P, R], U8, name="ws_dealt", align_bytes=64)
-        x_got = sbuf.tile([P, J], U32, name="x_got", align_bytes=64)
-        xs_got = sbuf.tile([P, J], U8, name="xs_got", tag="got_scales", align_bytes=64)
-        a_sb = [sbuf.tile([P, J], F32, name="a_sb%d" % t, tag="rows%d" % t, align_bytes=64) for t in range(PACK)]
+        w_dealt = d_room.tile([P, 2 * R], U8, name="w_dealt", offset=1536, align_bytes=64)
+        x_got = sbuf.tile([P, J], U32, name="x_got", tag="x_got", align_bytes=64)
+        a_sb = [sbuf.tile([P, J], F32, name="a_sb%d" % t, tag="rows%d" % t) for t in range(PACK)]
+        ws_dealt = [sbuf.tile([P, 2, P], U8, name="ws_dealt0", align_bytes=64)]
+        xs_got = [sbuf.tile([P, HALF], U8, name="xs_got0", tag="got_scales", align_bytes=64)]
 
-        def deal(t0, t1):
+        def deal_words(t0, t1):
             nc.scalar.copy(
                 w_dealt[:].bitcast(U16).rearrange("p (t m) -> p t m", t=PACK)[:, t0:t1, :],
                 w_raw[:].bitcast(U16).rearrange("p (m t) -> p t m", t=PACK)[:, t0:t1, :],
             )
+
+        def deal_scales(pair):
             nc.vector.tensor_copy(
-                ws_dealt[:].rearrange("p (t m) -> p t m", t=PACK)[:, t0:t1, :],
-                ws_plane[:].rearrange("p (m t) -> p t m", t=PACK)[:, t0:t1, :],
+                ws_dealt[pair][:], ws_plane[:].rearrange("p (m t) -> p t m", t=PACK)[:, 2 * pair : 2 * pair + 2, :]
             )
 
-        def gather_tokens(lo, hi):
-            at = tokens[:, lo // 16 : hi // 16]
-            nc.vector.tensor_copy(xs_got[:, lo:hi], xs_plane[:].indirect(at))
-            nc.vector.tensor_copy(x_got[:, lo:hi], x_raw[:].bitcast(U32).indirect(at))
+        def gather_tokens(half):
+            at = tokens[:, half * HALF // 16 : (half + 1) * HALF // 16]
+            nc.vector.tensor_copy(xs_got[half][:], xs_plane[:].indirect(at))
+            nc.vector.tensor_copy(x_got[:, half * HALF : (half + 1) * HALF], x_raw[:].bitcast(U32).indirect(at))
 
-        def first_product(t, lo, hi, emptier):
-            acc = psum.tile([P, hi - lo], F32, name="acc%d_%d" % (t, lo))
-            nc.tensor.matmul_mx(
-                out=acc[:],
-                lhsT=w_dealt[:, 2 * P * t : 2 * P * (t + 1)].bitcast(E2M1X4),
-                lhsT_scale=ws_dealt[:, P * t : P * (t + 1)],
-                rhs=x_got[:, lo:hi].bitcast(E4M3X4),
-                rhs_scale=xs_got[:, lo:hi],
-                start=True,
-                stop=True,
-            )
-            emptier(a_sb[t][:, lo:hi], acc[:])
+        def first_product(t, halves, emptier):
+            acc = psum.tile([P, len(halves), HALF], F32, name="acc%d_%d" % (t, halves[0]))
+            for slot, half in enumerate(halves):
+                nc.tensor.matmul_mx(
+                    out=acc[:, slot, :],
+                    lhsT=w_dealt[:, 2 * P * t : 2 * P * (t + 1)].bitcast(E2M1X4),
+                    lhsT_scale=ws_dealt[t // 2][:, t % 2, :],
+                    rhs=x_got[:, half * HALF : (half + 1) * HALF].bitcast(E4M3X4),
+                    rhs_scale=xs_got[half][:],
+                    start=True,
+                    stop=True,
+                )
+            emptier(a_sb[t][:, halves[0] * HALF : (halves[-1] + 1) * HALF], acc[:].rearrange("p h j -> p (h j)"))
 
         def put_on_board(t, lo, hi):
             nc.scalar.activation(boards[t][:].indirect(put[:, lo // 16 : hi // 16]), a_sb[t][:, lo:hi], COPY)
 
-        deal(0, 2)
-        gather_tokens(0, HALF)
+        deal_scales(0)
+        gather_tokens(0)
         for t in range(2):
-            first_product(t, 0, HALF, nc.scalar.copy)
-        gather_tokens(HALF, J)
-        deal(2, PACK)
+            deal_words(t, t + 1)
+        deal_words(2, PACK)
+        for t in range(2):
+            first_product(t, [0], nc.scalar.copy)
+        xs_got.append(w_room.tile([P, HALF], U8, name="xs_got1", offset=0, align_bytes=64))
+        ws_dealt.append(w_room.tile([P, 2, P], U8, name="ws_dealt1", offset=HALF, align_bytes=64))
+        gather_tokens(1)
+        deal_scales(1)
         for t in range(2):
             put_on_board(t, 0, HALF)
         for t in range(2):
-            first_product(t, HALF, J, nc.vector.tensor_copy)
+            first_product(t, [1], nc.vector.tensor_copy)
             put_on_board(t, HALF, J)
         for t in range(2, PACK):
-            first_product(t, 0, J, nc.vector.tensor_copy)
-            clear_board(x_room.tile([P, C], F32, name="board%d" % t, offset=4 * C * (t - 2)), nc.gpsimd)
+            first_product(t, [0, 1], nc.vector.tensor_copy)
+        for t in range(2, PACK):
+            clear_board(d_room.tile([P, C], F32, name="board%d" % t, offset=4 * C * (t - 2)))
+            put_on_board(t, 0, J)
 
-        v_got = sbuf.tile([P, N], U32, name="v_got", tag="vs_plane", align_bytes=64)
+        pages = []
+
+        def clear_page(page):
+            nc.vector.memset(page[:], 0.0)
+            pages.append(page)
+
+        clear_page(sbuf.tile([P, E], F32, name="page0", tag="x_got", align_bytes=64))
+        for t in range(2):
+            clear_page(sbuf.tile([P, E], F32, name="page%d" % (t + 1), tag="rows%d" % t))
         vs_got = sbuf.tile([P, N], U8, name="vs_got", tag="got_scales", align_bytes=64)
+        v_got = s_room.tile([P, N], U32, name="v_got", offset=0, align_bytes=64)
         nc.vector.tensor_copy(vs_got[:], vs_plane[:].indirect(entries[:]))
         nc.vector.tensor_copy(v_got[:], v_raw[:].bitcast(U32).indirect(entries[:]))
 
         hid = sbuf.tile([P, O, PACK], BF16, name="hid", align_bytes=64)
-        pages = []
-
-        def clear_page(page):
-            nc.gpsimd.memset(page[:], 0.0)
-            pages.append(page)
+        clear_page(s_room.tile([P, E], F32, name="page3", offset=1024))
 
         def read_board(t):
             left = v_room.tile([P, O], F32, name="left%d" % t, offset=4 * O * 2 * t)
@@ -178,12 +194,6 @@ def tile_list_ownreads_solo_store_owntwopages_kernel(
             pairs = gaps[:].rearrange("p t o -> p o t")[:, cols, :]
             nc.vector.scalar_tensor_tensor(hid[:, cols, t0 : t0 + 2], pairs, -1.0, pairs, ALU.mult, ALU.max)
 
-        clear_page(x_room.tile([P, E], F32, name="page0", offset=2 * 4 * C))
-        for t in range(2):
-            clear_page(sbuf.tile([P, E], F32, name="page%d" % (t + 1), tag="rows%d" % t, align_bytes=64))
-        put_on_board(2, 0, J)
-        clear_page(sbuf.tile([P, E], F32, name="page3", tag="rows2", align_bytes=64))
-        put_on_board(3, 0, J)
         whole = slice(0, O)
         halves = (slice(0, O // 2), slice(O // 2, O))
         gaps = sbuf.tile([P, 2, O], F32, name="gaps01", tag="gaps")

@@ -41,35 +41,34 @@ def tile_list_ownreads_solo_store_owntwopages_kernel(
             nc.sync.dma_start(tile[:], source)
             return tile
 
-        def load_scale_rows(name, source, queues):
+        def load_scale_rows(name, source, queue):
             width = source.shape[2] // 4
             staged = sbuf.tile([P, 2, width], I32, name=name)
             rows = source[0].bitcast(I32)
-            for h in range(2):
-                queues[h].dma_start(
+            for h in (1, 0):
+                queue.dma_start(
                     staged[64 * h : 64 * h + 4, :, :],
                     rows[8 * h : 8 * h + 8, :].rearrange("(q r) n -> r q n", q=2),
                 )
             return staged
 
-        def spread_scale_rows(name, staged, in_place_copy):
-            width = staged.shape[2]
-            plane = sbuf.tile([P, 4 * width], U8, name=name, tag=name, align_bytes=64)
+        def cleared_plane(name, width):
+            plane = sbuf.tile([P, width], U8, name=name, align_bytes=64)
             nc.vector.memset(plane[:].bitcast(I32), 0)
-            for h in range(2):
-                rows = slice(64 * h, 64 * h + 4)
-                in_place_copy(plane[:].bitcast(U32)[rows, :], staged[rows, 0, :].bitcast(U32))
-                nc.vector.tensor_copy(plane[:].bitcast(I32)[64 * h + 32 : 64 * h + 36, :], staged[rows, 1, :])
             return plane
+
+        def spread_quadrant(q, plane, staged):
+            first = 64 * (q // 2)
+            nc.vector.tensor_copy(plane[:].bitcast(I32)[32 * q : 32 * q + 4, :], staged[first : first + 4, q % 2, :])
 
         def load_words(name, source, room, offset):
             tile = room.tile([P, source.shape[2]], I32, name=name, offset=offset)
             nc.sync.dma_start(tile[:], source[0].rearrange("p n t -> p (n t)").bitcast(I32))
             return tile
 
+        xs_staged = load_scale_rows("xs_staged", xt_scales, nc.scalar)
+        ws_staged = load_scale_rows("ws_staged", w_scales, nc.sync)
         tokens = load_list("tokens", offs)
-        ws_staged = load_scale_rows("ws_staged", w_scales, (nc.scalar, nc.sync))
-        xs_staged = load_scale_rows("xs_staged", xt_scales, (nc.scalar, nc.sync))
         x_raw = load_words("x_raw", xt_words, sbuf, None)
         w_raw = w_room.tile([P, 2 * R], U8, name="w_raw", offset=0)
         nc.sync.dma_start(w_raw[:].bitcast(I32), w_words[0].bitcast(I32))
@@ -91,8 +90,11 @@ def tile_list_ownreads_solo_store_owntwopages_kernel(
         own = load_list("own", offs6)
         common = load_list("common", offs7)
 
-        ws_plane = spread_scale_rows("ws_plane", ws_staged, nc.vector.tensor_copy)
-        xs_plane = spread_scale_rows("xs_plane", xs_staged, nc.vector.tensor_copy)
+        xs_plane = cleared_plane("xs_plane", T)
+        ws_plane = cleared_plane("ws_plane", R)
+        for q in (2, 3, 1, 0):
+            spread_quadrant(q, ws_plane, ws_staged)
+            spread_quadrant(q, xs_plane, xs_staged)
         boards = []
 
         def clear_board(board):

from contextlib import ExitStack

import concourse.mybir as mybir

K, T, J, R, C, O, N, S, E = 512, 1024, 256, 512, 512, 128, 256, 1024, 512
FLOPS = 2 * K * R * J + 2 * R * N * O

F32 = mybir.dt.float32
BF16 = mybir.dt.bfloat16
I32 = mybir.dt.int32
U32 = mybir.dt.uint32
U16 = mybir.dt.uint16
U8 = mybir.dt.uint8
E4M3X4 = mybir.dt.float8_e4m3fn_x4
E5M2X4 = mybir.dt.float8_e5m2_x4
E2M1X4 = mybir.dt.float4_e2m1fn_x4
ALU = mybir.AluOpType
COPY = mybir.ActivationFunctionType.Copy

P = 128
PACK = 4
HALF = J // 2


def tile_list_ownreads_solo_store_owntwopages_kernel(
    tc, xt_words, xt_scales, w_words, w_scales, sa, sb, vs_words, vs_scales,
    offs, offs2, offs3, offs4, offs5, offs6, offs7, out,
):
    nc = tc.nc
    with ExitStack() as ctx:
        lists = ctx.enter_context(tc.tile_pool(name="lists", bufs=1))
        sbuf = ctx.enter_context(tc.tile_pool(name="sbuf", bufs=1))
        w_room = ctx.enter_context(tc.tile_pool(name="w_room", bufs=1))
        d_room = ctx.enter_context(tc.tile_pool(name="d_room", bufs=1))
        s_room = ctx.enter_context(tc.tile_pool(name="s_room", bufs=1))
        v_room = ctx.enter_context(tc.tile_pool(name="v_room", bufs=1))
        psum = ctx.enter_context(tc.psum_pool(name="psum", bufs=1))

        def load_list(name, source):
            tile = lists.tile([P, source.shape[1]], U16, name=name)
            nc.sync.dma_start(tile[:], source)
            return tile

        def load_scale_rows(name, source, queue):
            width = source.shape[2] // 4
            staged = sbuf.tile([P, 2, width], I32, name=name)
            rows = source[0].bitcast(I32)
            for h in (1, 0):
                queue.dma_start(
                    staged[64 * h : 64 * h + 4, :, :],
                    rows[8 * h : 8 * h + 8, :].rearrange("(q r) n -> r q n", q=2),
                )
            return staged

        def cleared_plane(name, width):
            plane = sbuf.tile([P, width], U8, name=name, align_bytes=64)
            nc.vector.memset(plane[:].bitcast(I32), 0)
            return plane

        def spread_quadrant(q, plane, staged):
            first = 64 * (q // 2)
            nc.vector.tensor_copy(plane[:].bitcast(I32)[32 * q : 32 * q + 4, :], staged[first : first + 4, q % 2, :])

        def load_words(name, source, room, offset):
            tile = room.tile([P, source.shape[2]], I32, name=name, offset=offset)
            nc.sync.dma_start(tile[:], source[0].rearrange("p n t -> p (n t)").bitcast(I32))
            return tile

        xs_staged = load_scale_rows("xs_staged", xt_scales, nc.scalar)
        ws_staged = load_scale_rows("ws_staged", w_scales, nc.sync)
        tokens = load_list("tokens", offs)
        x_raw = load_words("x_raw", xt_words, sbuf, None)
        w_raw = w_room.tile([P, 2 * R], U8, name="w_raw", offset=0)
        nc.sync.dma_start(w_raw[:].bitcast(I32), w_words[0].bitcast(I32))
        put = load_list("put", offs2)
        pick_a = load_list("pick_a", offs3)
        pick_b = load_list("pick_b", offs4)
        sa_sb = sbuf.tile([P, PACK], F32, name="sa_sb")
        sb_sb = sbuf.tile([P, PACK], F32, name="sb_sb")
        nc.sync.dma_start(sa_sb[:], sa.rearrange("(p t) o -> p (t o)", t=PACK))
        nc.sync.dma_start(sb_sb[:], sb.rearrange("(p t) o -> p (t o)", t=PACK))
        entries = load_list("entries", offs5)
        vs_plane = s_room.tile([P, S], U8, name="vs_plane", offset=512, align_bytes=64)
        nc.vector.memset(vs_plane[:].bitcast(I32), 0)
        for q in range(4):
            nc.sync.dma_start(
                vs_plane[:].bitcast(I32)[32 * q : 32 * q + 4, :], vs_scales[0].bitcast(I32)[4 * q : 4 * q + 4, :]
            )
        v_raw = load_words("v_raw", vs_words, v_room, 0)
        own = load_list("own", offs6)
        common = load_list("common", offs7)

        xs_plane = cleared_plane("xs_plane", T)
        ws_plane = cleared_plane("ws_plane", R)
        for q in (2, 3, 1, 0):
            spread_quadrant(q, ws_plane, ws_staged)
            spread_quadrant(q, xs_plane, xs_staged)
        boards = []

        def clear_board(board):
            nc.vector.memset(board[:], 0.0)
            boards.append(board)

        for t in range(2):
            clear_board(sbuf.tile([P, C], F32, name="board%d" % t))

        w_dealt = d_room.tile([P, 2 * R], U8, name="w_dealt", offset=1536, align_bytes=64)
        x_got = sbuf.tile([P, J], U32, name="x_got", tag="x_got", align_bytes=64)
        a_sb = [sbuf.tile([P, J], F32, name="a_sb%d" % t, tag="rows%d" % t) for t in range(PACK)]
        ws_dealt = [sbuf.tile([P, 2, P], U8, name="ws_dealt0", align_bytes=64)]
        xs_got = [sbuf.tile([P, HALF], U8, name="xs_got0", tag="got_scales", align_bytes=64)]

        def deal_words(t0, t1):
            nc.scalar.copy(
                w_dealt[:].bitcast(U16).rearrange("p (t m) -> p t m", t=PACK)[:, t0:t1, :],
                w_raw[:].bitcast(U16).rearrange("p (m t) -> p t m", t=PACK)[:, t0:t1, :],
            )

        def deal_scales(pair):
            nc.vector.tensor_copy(
                ws_dealt[pair][:], ws_plane[:].rearrange("p (m t) -> p t m", t=PACK)[:, 2 * pair : 2 * pair + 2, :]
            )

        def gather_tokens(half):
            at = tokens[:, half * HALF // 16 : (half + 1) * HALF // 16]
            nc.vector.tensor_copy(xs_got[half][:], xs_plane[:].indirect(at))
            nc.vector.tensor_copy(x_got[:, half * HALF : (half + 1) * HALF], x_raw[:].bitcast(U32).indirect(at))

        def first_product(t, halves, emptier):
            acc = psum.tile([P, len(halves), HALF], F32, name="acc%d_%d" % (t, halves[0]))
            for slot, half in enumerate(halves):
                nc.tensor.matmul_mx(
                    out=acc[:, slot, :],
                    lhsT=w_dealt[:, 2 * P * t : 2 * P * (t + 1)].bitcast(E2M1X4),
                    lhsT_scale=ws_dealt[t // 2][:, t % 2, :],
                    rhs=x_got[:, half * HALF : (half + 1) * HALF].bitcast(E4M3X4),
                    rhs_scale=xs_got[half][:],
                    start=True,
                    stop=True,
                )
            emptier(a_sb[t][:, halves[0] * HALF : (halves[-1] + 1) * HALF], acc[:].rearrange("p h j -> p (h j)"))

        def put_on_board(t, lo, hi):
            nc.scalar.activation(boards[t][:].indirect(put[:, lo // 16 : hi // 16]), a_sb[t][:, lo:hi], COPY)

        deal_scales(0)
        gather_tokens(0)
        for t in range(2):
            deal_words(t, t + 1)
        deal_words(2, PACK)
        for t in range(2):
            first_product(t, [0], nc.scalar.copy)
        xs_got.append(w_room.tile([P, HALF], U8, name="xs_got1", offset=0, align_bytes=64))
        ws_dealt.append(w_room.tile([P, 2, P], U8, name="ws_dealt1", offset=HALF, align_bytes=64))
        gather_tokens(1)
        deal_scales(1)
        for t in range(2):
            put_on_board(t, 0, HALF)
        for t in range(2):
            first_product(t, [1], nc.vector.tensor_copy)
            put_on_board(t, HALF, J)
        for t in range(2, PACK):
            first_product(t, [0, 1], nc.vector.tensor_copy)
        for t in range(2, PACK):
            clear_board(d_room.tile([P, C], F32, name="board%d" % t, offset=4 * C * (t - 2)))
            put_on_board(t, 0, J)

        pages = []

        def clear_page(page):
            nc.vector.memset(page[:], 0.0)
            pages.append(page)

        clear_page(sbuf.tile([P, E], F32, name="page0", tag="x_got", align_bytes=64))
        for t in range(2):
            clear_page(sbuf.tile([P, E], F32, name="page%d" % (t + 1), tag="rows%d" % t))
        vs_got = sbuf.tile([P, N], U8, name="vs_got", tag="got_scales", align_bytes=64)
        v_got = s_room.tile([P, N], U32, name="v_got", offset=0, align_bytes=64)
        nc.vector.tensor_copy(vs_got[:], vs_plane[:].indirect(entries[:]))
        nc.vector.tensor_copy(v_got[:], v_raw[:].bitcast(U32).indirect(entries[:]))

        hid = sbuf.tile([P, O, PACK], BF16, name="hid", align_bytes=64)
        clear_page(s_room.tile([P, E], F32, name="page3", offset=1024))

        def read_board(t):
            left = v_room.tile([P, O], F32, name="left%d" % t, offset=4 * O * 2 * t)
            right = v_room.tile([P, O], F32, name="right%d" % t, offset=4 * O * (2 * t + 1))
            nc.scalar.activation(left[:], boards[t][:].indirect(pick_a[:]), COPY, scale=sa_sb[:, t : t + 1])
            nc.scalar.activation(right[:], boards[t][:].indirect(pick_b[:]), COPY, scale=sb_sb[:, t : t + 1])
            return left, right

        def difference(t, gaps, picked, cols):
            nc.vector.tensor_tensor(gaps[:, t % 2, cols], picked[0][:, cols], picked[1][:, cols], ALU.subtract)

        def magnitudes(t0, gaps, cols):
            pairs = gaps[:].rearrange("p t o -> p o t")[:, cols, :]
            nc.vector.scalar_tensor_tensor(hid[:, cols, t0 : t0 + 2], pairs, -1.0, pairs, ALU.mult, ALU.max)

        whole = slice(0, O)
        halves = (slice(0, O // 2), slice(O // 2, O))
        gaps = sbuf.tile([P, 2, O], F32, name="gaps01", tag="gaps")
        for t in range(2):
            difference(t, gaps, read_board(t), whole)
        magnitudes(0, gaps, whole)
        gaps = sbuf.tile([P, 2, O], F32, name="gaps23", tag="gaps")
        difference(2, gaps, read_board(2), whole)
        picked = read_board(3)
        hid_codes = sbuf.tile([P, O], U32, name="hid_codes", align_bytes=64)
        hid_scales = sbuf.tile([P, O], U8, name="hid_scales", align_bytes=64)
        for cols in halves:
            difference(3, gaps, picked, cols)
        for cols in halves:
            magnitudes(2, gaps, cols)
        for cols in halves:
            nc.vector.quantize_mx(
                out=hid_codes[:, cols].bitcast(E4M3X4),
                scales=hid_scales[:, cols],
                in_=hid[:, cols, :].rearrange("p o t -> p (o t)"),
            )

        results = []
        for c, emptier in enumerate((nc.scalar.copy, nc.vector.tensor_copy)):
            acc = psum.tile([P, O], F32, name="res%d" % c)
            nc.tensor.matmul_mx(
                out=acc[:],
                lhsT=v_got[:, P * c : P * (c + 1)].bitcast(E5M2X4),
                lhsT_scale=vs_got[:, P * c : P * (c + 1)],
                rhs=hid_codes[:].bitcast(E4M3X4),
                rhs_scale=hid_scales[:],
                start=True,
                stop=True,
            )
            result = sbuf.tile([P, O], F32, name="result%d" % c)
            emptier(result[:], acc[:])
            results.append(result)
        totals = [sbuf.tile([P, E], F32, name="total%d" % c) for c in range(2)]

        def add_and_store(c, pieces):
            for lo in range(0, E, E // pieces):
                cols = slice(lo, lo + E // pieces)
                nc.vector.tensor_tensor(totals[c][:, cols], pages[2 * c][:, cols], pages[2 * c + 1][:, cols], ALU.add)
                nc.sync.dma_start(out[P * c : P * (c + 1), cols], totals[c][:, cols])

        nc.scalar.activation(pages[0][:].indirect(own[:]), results[0][:], COPY)
        nc.vector.tensor_copy(pages[1][:].indirect(common[:]), results[0][:])
        nc.vector.tensor_copy(pages[3][:].indirect(common[:, 0:4]), results[1][:, 0:64])
        nc.scalar.activation(pages[2][:].indirect(own[:]), results[1][:], COPY)
        nc.scalar.activation(pages[3][:].indirect(common[:, 4:8]), results[1][:, 64:128], COPY)
        add_and_store(0, 1)
        add_and_store(1, 2)
